import numpy as np, ml_dtypes
CORES = [32,40,48,56,64,72,80,88,96,104,112,120]
N = 12
TK = 256
def silu(z): return z / (1.0 + np.exp(-z))
WID = [32,192,256,64,96,64,96,64,192,64,192,96]
def setup_inputs(rng):
    return {"x": rng.standard_normal((N, 128, TK), dtype=np.float32).astype(ml_dtypes.bfloat16), "w1": (rng.standard_normal((N, 128, 128), dtype=np.float32) / 8).astype(ml_dtypes.bfloat16), "w3": (rng.standard_normal((N, 128, 128), dtype=np.float32) / 8).astype(ml_dtypes.bfloat16), "w2": (rng.standard_normal((N, 128, 128), dtype=np.float32) / 8).astype(ml_dtypes.bfloat16)}
def setup_inputs_big(rng):
    d = setup_inputs(rng)
    for k in ("x",): d[k] = (d[k].astype(np.float32) * 1024.0).astype(d[k].dtype)
    return d
def setup_inputs_small(rng):
    d = setup_inputs(rng)
    for k in ("x",): d[k] = (d[k].astype(np.float32) * (1 / 1024.0)).astype(d[k].dtype)
    return d
def setup_inputs_apart(rng):
    d = setup_inputs(rng)
    f = (10.0 ** rng.permutation(np.linspace(-1.5, 1.5, N))).astype(np.float32).reshape(N, 1, 1)
    for k in ("x",): d[k] = (d[k].astype(np.float32) * f).astype(d[k].dtype)
    return d
def whole(x, w1, w3, w2):
    X, W1, W3, W2 = x.astype(np.float64), w1.astype(np.float64), w3.astype(np.float64), w2.astype(np.float64)
    y = np.zeros((N, 128, TK))
    for r in range(N):
        for j in range(N):
            y[r] += W2[j].T @ (silu(W1[j].T @ X[r]) * (W3[j].T @ X[r]))
    return {"y": y.astype(ml_dtypes.bfloat16)}
def reference(x, w1, w3, w2):
    o = whole(x, w1, w3, w2)["y"].copy()
    for r in range(N):
        o[r][:, WID[r]:] = np.nan
    return {"y": o}

@@ -1,0 +1,241 @@
+from concourse.bass import DstId, RemoteDMATransfer
+from concourse.mybir import AluOpType, ActivationFunctionType
+import comms_topo
+
+CORES = [32, 40, 48, 56, 64, 72, 80, 88, 96, 104, 112, 120]
+D = 128
+TK = 256
+NC = 3
+FWD = {4: 0, 5: 1}
+NSET = 1 + sum(1 for c in CORES[1:] if comms_topo.same_plane(comms_topo.chip(CORES[0]), comms_topo.chip(c)))
+SLOTS = NSET // NC
+NU = 2 * SLOTS
+
+SCRATCH = {
+    "x0": ("sbuf", [D, TK], "bfloat16"),
+    "wown": ("sbuf", [D, 3 * D], "bfloat16"),
+    "ones": ("sbuf", [D, D], "bfloat16"),
+    "ident": ("sbuf", [D, D], "bfloat16"),
+    "yout": ("sbuf", [D, TK], "bfloat16"),
+    "yacc": ("psum", [D, 512], "float32"),
+    "xo": ("sbuf", [D, TK], "bfloat16"),
+    "xm": ("sbuf", [D, TK], "bfloat16"),
+    "yb0": ("sbuf", [D, TK], "bfloat16"),
+    "yb1": ("sbuf", [D, TK], "bfloat16"),
+    "z10": ("psum", [D, 512], "float32"),
+    "z11": ("psum", [D, 512], "float32"),
+    "z30": ("psum", [D, 512], "float32"),
+    "z31": ("psum", [D, 512], "float32"),
+    "yp0": ("psum", [D, 512], "float32"),
+    "yp1": ("psum", [D, 512], "float32"),
+}
+for _i in range(2 * NC):
+    SCRATCH["part%d" % _i] = ("sbuf", [D, TK], "bfloat16")
+for _i in range(SLOTS):
+    SCRATCH["wl%d" % _i] = ("sbuf", [D, 3 * D], "bfloat16")
+for _i in range(NU):
+    SCRATCH["s%d" % _i] = ("sbuf", [D, TK], "float32")
+    SCRATCH["h%d" % _i] = ("sbuf", [D, TK], "bfloat16")
+
+SEMAPHORES = (["lx", "lw", "idm", "ids", "snt", "acc", "cp", "st", "xo", "xm",
+               "z1s", "z3s", "ss", "hs", "ys", "yca", "ycb"]
+              + ["pa%d" % i for i in range(2 * NC)] + ["ws%d" % i for i in range(SLOTS)])
+
+
+def _bits(m):
+    return bin(m).count("1")
+
+
+def _plan(T, topo):
+    cores = list(T.cores)
+    info = {}
+    for r, R in enumerate(cores):
+        ch = topo.chip(R)
+        mate = [q for q in cores if topo.mates(ch, topo.chip(q))][0]
+        plane = [q for q in cores if q == R or topo.same_plane(ch, topo.chip(q))]
+        own = [c for c in range(topo.CHIPS * topo.CORES_PER_CHIP)
+               if topo.chip(c) == ch and c != R and topo.may_write(c, mate)]
+        own.sort(key=lambda c: (topo.die(c) == topo.die(R), c))
+        info[R] = {"rank": r, "mate": mate, "plane": plane, "comp": own[:NC]}
+    return info
+
+
+def _where(info, plane, j, s):
+    q = plane[(j + s) % len(plane)]
+    return info[q]["comp"][s % NC], s // NC
+
+
+def _wmask(info, topo, plane, j, s):
+    dst = _where(info, plane, j, s)[0]
+    if s == 0:
+        return topo.mask(plane[j], dst) & ~topo.mask(plane[j], info[plane[j]]["mate"])
+    src = _where(info, plane, j, FWD[s])[0] if s in FWD else plane[j]
+    return topo.mask(src, dst)
+
+
+def _send(g, topo, dst, out_ap, in_ap, rsem, lsem, mask, sent):
+    rid, pid, _ = topo.addr(dst)
+    g.remote_dma(out_ap=out_ap, in_ap=in_ap, remote_sem=rsem, local_sem=lsem, pid=pid, routing_id=rid,
+                 dma_engine_mask=mask)
+    sent[0] += _bits(mask)
+
+
+def _rank_core(g, R, T, topo, info):
+    S = T.sem
+    me = info[R]
+    wid = T.tables["WID"][me["rank"]]
+    comp, plane = me["comp"], me["plane"]
+    n, p = len(plane), plane.index(R)
+    sent = [0]
+
+    g.sync.dma_start(T.x0[:, :wid], T.x[:, :wid]).then_inc(S.lx, 16)
+    g.scalar.dma_start(T.wown[:, 0:D], T.w1[:, :]).then_inc(S.lw, 16)
+    g.sync.dma_start(T.wown[:, D:2 * D], T.w3[:, :]).then_inc(S.lw, 16)
+    g.scalar.dma_start(T.wown[:, 2 * D:3 * D], T.w2[:, :]).then_inc(S.lw, 16)
+
+    g.vector.memset(T.ones[:, :], 1.0).then_inc(S.idm, 1)
+    g.wait_ge(S.idm, 1)
+    g.affine_select(T.ident[:, :], T.ones[:, :], [[-1, D]], AluOpType.is_equal, 0.0, 0, 1).then_inc(S.ids, 1)
+
+    xmask = topo.mask(R, comp[0]) & topo.mask(R, me["mate"])
+    g.wait_ge(S.lx, 16)
+    ids = []
+    for c in comp:
+        rid, pid, _ = topo.addr(c)
+        ids.append(DstId(rid=rid, pnc=pid))
+    g.remote_dma_fused([RemoteDMATransfer(dst_ids=ids, dma_engine_mask=xmask, remote_sem=S.xo,
+                                          srcs=[T.x0[:, :wid]], dsts=[T.xo[:, :wid]] * len(comp))],
+                       local_sem=S.snt)
+    sent[0] += _bits(xmask)
+
+    g.wait_ge(S.lw, 48)
+    direct = [s for s in range(1, n) if s not in FWD]
+    trs = []
+    for s in (0, direct[0]):
+        c, sl = _where(info, plane, p, s)
+        rid, pid, _ = topo.addr(c)
+        m = _wmask(info, topo, plane, p, s)
+        trs.append(RemoteDMATransfer(dst_ids=[DstId(rid=rid, pnc=pid)], dma_engine_mask=m,
+                                     remote_sem=S["ws%d" % sl], srcs=[T.wown[:, :]], dsts=[T["wl%d" % sl][:, :]]))
+        sent[0] += _bits(m)
+    g.remote_dma_fused(trs, local_sem=S.snt)
+    for s in direct[1:]:
+        c, sl = _where(info, plane, p, s)
+        _send(g, topo, c, T["wl%d" % sl][:, :], T.wown[:, :], S["ws%d" % sl], S.snt,
+              _wmask(info, topo, plane, p, s), sent)
+
+    g.tensor.wait_ge(S.ids, 1)
+    for i in range(2 * NC):
+        k, far = i // 2, i % 2
+        src = info[me["mate"]]["comp"][k] if far else comp[k]
+        g.tensor.wait_ge(S["pa%d" % i], _bits(_ymask(topo, info, src)))
+        mm = g.tensor.matmul(T.yacc[:, :wid], T.ident[:, :], T["part%d" % i][:, :wid], i == 0, i == 2 * NC - 1)
+    mm.then_inc(S.acc, 1)
+    g.vector.wait_ge(S.acc, 1)
+    g.vector.tensor_copy(T.yout[:, :wid], T.yacc[:, :wid]).then_inc(S.cp, 1)
+    g.sync.wait_ge(S.cp, 1)
+    g.sync.dma_start(T.y[:, :wid], T.yout[:, :wid]).then_inc(S.st, 16)
+    g.sync.wait_ge(S.st, 16)
+    g.wait_ge(S.snt, sent[0])
+
+
+def _home(topo, info, c):
+    return [R for R in info if topo.chip(R) == topo.chip(c)][0]
+
+
+def _ymask(topo, info, c):
+    R = _home(topo, info, c)
+    return topo.mask(c, R) & topo.mask(c, info[R]["mate"])
+
+
+def _compute_core(g, c, T, topo, info):
+    S = T.sem
+    R = _home(topo, info, c)
+    me = info[R]
+    k = me["comp"].index(c)
+    plane = me["plane"]
+    n, p = len(plane), plane.index(R)
+    mateR = me["mate"]
+    peer = info[mateR]["comp"][k]
+    wid = (T.tables["WID"][me["rank"]], T.tables["WID"][info[mateR]["rank"]])
+    X = (T.xo, T.xm)
+    YP = (T.yp0, T.yp1)
+    YB = (T.yb0, T.yb1)
+    ym = _ymask(topo, info, c)
+    xcnt = (_bits(topo.mask(R, c) & topo.mask(R, mateR)), _bits(_ymask(topo, info, peer)))
+    xsem = (S.xo, S.xm)
+    wcnt = [_bits(_wmask(info, topo, plane, (p - (sl * NC + k)) % n, sl * NC + k)) for sl in range(SLOTS)]
+    sent = [0]
+
+    big = 0 if wid[0] >= wid[1] else 1
+    units = []
+    for sl in range(SLOTS):
+        first = big if sl == SLOTS - 1 else 0
+        units += [(sl, first), (sl, 1 - first)]
+
+    g.wait_ge(S.xo, xcnt[0])
+    _send(g, topo, peer, T.xm[:, :wid[0]], T.xo[:, :wid[0]], S.xm, S.snt, ym, sent)
+    for sl in range(SLOTS):
+        held = sl * NC + k
+        j = (p - held) % n
+        for s in sorted(FWD):
+            if FWD[s] == held:
+                dst, dsl = _where(info, plane, j, s)
+                g.wait_ge(S["ws%d" % sl], wcnt[sl])
+                _send(g, topo, dst, T["wl%d" % dsl][:, :], T["wl%d" % sl][:, :], S["ws%d" % dsl], S.snt,
+                      _wmask(info, topo, plane, j, s), sent)
+    for q, sem in ((big, S.yca), (1 - big, S.ycb)):
+        g.wait_ge(sem, 1)
+        dst = mateR if q else R
+        i = 2 * k + q
+        _send(g, topo, dst, T["part%d" % i][:, :wid[q]], YB[q][:, :wid[q]], S["pa%d" % i], S.snt, ym, sent)
+    g.wait_ge(S.snt, sent[0])
+
+    def z(u):
+        sl, q = units[u]
+        w, b = wid[q], u % 2
+        g.tensor.wait_ge(xsem[q], xcnt[q])
+        g.tensor.wait_ge(S["ws%d" % sl], wcnt[sl])
+        if u >= 2:
+            g.tensor.wait_ge(S.hs, u - 1)
+        W = T["wl%d" % sl]
+        g.tensor.matmul(T["z1%d" % b][:, :w], W[:, 0:D], X[q][:, :w], True, True).then_inc(S.z1s, 1)
+        g.tensor.matmul(T["z3%d" % b][:, :w], W[:, D:2 * D], X[q][:, :w], True, True).then_inc(S.z3s, 1)
+
+    def y(u):
+        sl, q = units[u]
+        w = wid[q]
+        g.tensor.wait_ge(S.hs, u + 1)
+        g.tensor.matmul(YP[q][:, :w], T["wl%d" % sl][:, 2 * D:3 * D], T["h%d" % u][:, :w],
+                        sl == 0, sl == SLOTS - 1).then_inc(S.ys, 1)
+
+    for sl in range(SLOTS):
+        z(2 * sl)
+        z(2 * sl + 1)
+        y(2 * sl)
+        y(2 * sl + 1)
+
+    for u in range(NU):
+        sl, q = units[u]
+        w, b = wid[q], u % 2
+        g.scalar.wait_ge(S.z1s, u + 1)
+        g.scalar.activation(T["s%d" % u][:, :w], T["z1%d" % b][:, :w], ActivationFunctionType.Silu).then_inc(S.ss, 1)
+        g.vector.wait_ge(S.ss, u + 1)
+        g.vector.wait_ge(S.z3s, u + 1)
+        g.vector.tensor_tensor(T["h%d" % u][:, :w], T["s%d" % u][:, :w], T["z3%d" % b][:, :w],
+                               AluOpType.mult).then_inc(S.hs, 1)
+    g.scalar.wait_ge(S.ys, NU - 1)
+    g.scalar.activation(YB[big][:, :wid[big]], YP[big][:, :wid[big]], ActivationFunctionType.Copy).then_inc(S.yca, 1)
+    g.vector.wait_ge(S.ys, NU)
+    g.vector.tensor_copy(YB[1 - big][:, :wid[1 - big]], YP[1 - big][:, :wid[1 - big]]).then_inc(S.ycb, 1)
+
+
+def rank_program(g, core, T, topo):
+    info = _plan(T, topo)
+    if core in info:
+        _rank_core(g, core, T, topo, info)
+        return
+    for R in info:
+        if core in info[R]["comp"]:
+            _compute_core(g, core, T, topo, info)
+            return

@@ -6,6 +6,7 @@ CORES = [32, 40, 48, 56, 64, 72, 80, 88, 96, 104, 112, 120]
 D = 128
 TK = 256
 NC = 3
+IB = D // (NC + 1)
 FWD = {4: 0, 5: 1}
 NSET = 1 + sum(1 for c in CORES[1:] if comms_topo.same_plane(comms_topo.chip(CORES[0]), comms_topo.chip(c)))
 SLOTS = NSET // NC
@@ -14,19 +15,15 @@ NU = 2 * SLOTS
 SCRATCH = {
     "x0": ("sbuf", [D, TK], "bfloat16"),
     "wown": ("sbuf", [D, 3 * D], "bfloat16"),
-    "ones": ("sbuf", [D, D], "bfloat16"),
     "ident": ("sbuf", [D, D], "bfloat16"),
     "yout": ("sbuf", [D, TK], "bfloat16"),
-    "yacc": ("psum", [D, 512], "float32"),
+    "ones": ("sbuf", [D, IB], "bfloat16"),
+    "idb": ("sbuf", [D, IB], "bfloat16"),
+    "yp0": ("psum", [D, 512], "float32"),
     "xo": ("sbuf", [D, TK], "bfloat16"),
     "xm": ("sbuf", [D, TK], "bfloat16"),
     "yb0": ("sbuf", [D, TK], "bfloat16"),
     "yb1": ("sbuf", [D, TK], "bfloat16"),
-    "z10": ("psum", [D, 512], "float32"),
-    "z11": ("psum", [D, 512], "float32"),
-    "z30": ("psum", [D, 512], "float32"),
-    "z31": ("psum", [D, 512], "float32"),
-    "yp0": ("psum", [D, 512], "float32"),
     "yp1": ("psum", [D, 512], "float32"),
 }
 for _i in range(2 * NC):
@@ -34,10 +31,15 @@ for _i in range(2 * NC):
 for _i in range(SLOTS):
     SCRATCH["wl%d" % _i] = ("sbuf", [D, 3 * D], "bfloat16")
 for _i in range(NU):
+    if _i < NU - 2:
+        SCRATCH["zz%d" % _i] = ("psum", [D, 512], "float32")
+    else:
+        SCRATCH["za%d" % _i] = ("psum", [D, 512], "float32")
+        SCRATCH["zb%d" % _i] = ("psum", [D, 512], "float32")
     SCRATCH["s%d" % _i] = ("sbuf", [D, TK], "float32")
     SCRATCH["h%d" % _i] = ("sbuf", [D, TK], "bfloat16")
 
-SEMAPHORES = (["lx", "lw", "idm", "ids", "snt", "acc", "cp", "st", "xo", "xm",
+SEMAPHORES = (["lx", "lw", "idm", "ids", "idr", "snt", "acc", "cp", "st", "xo", "xm",
                "z1s", "z3s", "ss", "hs", "ys", "yca", "ycb"]
               + ["pa%d" % i for i in range(2 * NC)] + ["ws%d" % i for i in range(SLOTS)])
 
@@ -80,6 +82,15 @@ def _send(g, topo, dst, out_ap, in_ap, rsem, lsem, mask, sent):
     sent[0] += _bits(mask)
 
 
+def _ident_block(g, me, T, topo, b, dst, sent):
+    S = T.sem
+    g.vector.memset(T.ones[:, :], 1.0).then_inc(S.idm, 1)
+    g.wait_ge(S.idm, 1)
+    g.affine_select(T.idb[:, :], T.ones[:, :], [[-1, IB]], AluOpType.is_equal, 0.0, -b * IB, 1).then_inc(S.ids, 1)
+    g.wait_ge(S.ids, 1)
+    _send(g, topo, dst, T.ident[:, b * IB:(b + 1) * IB], T.idb[:, :], S.idr, S.snt, topo.mask(me, dst), sent)
+
+
 def _rank_core(g, R, T, topo, info):
     S = T.sem
     me = info[R]
@@ -93,11 +104,9 @@ def _rank_core(g, R, T, topo, info):
     g.sync.dma_start(T.wown[:, D:2 * D], T.w3[:, :]).then_inc(S.lw, 16)
     g.scalar.dma_start(T.wown[:, 2 * D:3 * D], T.w2[:, :]).then_inc(S.lw, 16)
 
-    g.vector.memset(T.ones[:, :], 1.0).then_inc(S.idm, 1)
-    g.wait_ge(S.idm, 1)
-    g.affine_select(T.ident[:, :], T.ones[:, :], [[-1, D]], AluOpType.is_equal, 0.0, 0, 1).then_inc(S.ids, 1)
+    _ident_block(g, R, T, topo, NC, plane[(p + 1) % n], sent)
 
-    xmask = topo.mask(R, comp[0]) & topo.mask(R, me["mate"])
+    xmask = topo.mask(R, comp[0])
     g.wait_ge(S.lx, 16)
     ids = []
     for c in comp:
@@ -124,15 +133,20 @@ def _rank_core(g, R, T, topo, info):
         _send(g, topo, c, T["wl%d" % sl][:, :], T.wown[:, :], S["ws%d" % sl], S.snt,
               _wmask(info, topo, plane, p, s), sent)
 
-    g.tensor.wait_ge(S.ids, 1)
-    for i in range(2 * NC):
-        k, far = i // 2, i % 2
-        src = info[me["mate"]]["comp"][k] if far else comp[k]
-        g.tensor.wait_ge(S["pa%d" % i], _bits(_ymask(topo, info, src)))
-        mm = g.tensor.matmul(T.yacc[:, :wid], T.ident[:, :], T["part%d" % i][:, :wid], i == 0, i == 2 * NC - 1)
+    def _pcnt(i):
+        src = info[me["mate"]]["comp"][i // 2] if i % 2 else comp[i // 2]
+        return _bits(_pmask(topo, info, src, i % 2))
+
+    order = [2 * k for k in range(NC)] + [2 * k + 1 for k in range(NC)]
+    g.tensor.wait_ge(S.idr, sum(_bits(topo.mask(c, R)) for c in comp + [plane[(p - 1) % n]]))
+    for n_, i in enumerate(order[:-1]):
+        g.tensor.wait_ge(S["pa%d" % i], _pcnt(i))
+        mm = g.tensor.matmul(T.yp0[:, :wid], T.ident[:, :], T["part%d" % i][:, :wid], n_ == 0, n_ == len(order) - 2)
     mm.then_inc(S.acc, 1)
+    last = order[-1]
+    g.vector.wait_ge(S["pa%d" % last], _pcnt(last))
     g.vector.wait_ge(S.acc, 1)
-    g.vector.tensor_copy(T.yout[:, :wid], T.yacc[:, :wid]).then_inc(S.cp, 1)
+    g.vector.tensor_tensor(T.yout[:, :wid], T.yp0[:, :wid], T["part%d" % last][:, :wid], AluOpType.add).then_inc(S.cp, 1)
     g.sync.wait_ge(S.cp, 1)
     g.sync.dma_start(T.y[:, :wid], T.yout[:, :wid]).then_inc(S.st, 16)
     g.sync.wait_ge(S.st, 16)
@@ -146,6 +160,11 @@ def _home(topo, info, c):
 def _ymask(topo, info, c):
     R = _home(topo, info, c)
     return topo.mask(c, R) & topo.mask(c, info[R]["mate"])
+
+
+def _pmask(topo, info, c, far):
+    R = _home(topo, info, c)
+    return _ymask(topo, info, c) if far else topo.mask(c, R) & ~topo.mask(c, info[R]["mate"])
 
 
 def _compute_core(g, c, T, topo, info):
@@ -162,7 +181,7 @@ def _compute_core(g, c, T, topo, info):
     YP = (T.yp0, T.yp1)
     YB = (T.yb0, T.yb1)
     ym = _ymask(topo, info, c)
-    xcnt = (_bits(topo.mask(R, c) & topo.mask(R, mateR)), _bits(_ymask(topo, info, peer)))
+    xcnt = (_bits(topo.mask(R, c)), _bits(_ymask(topo, info, peer)))
     xsem = (S.xo, S.xm)
     wcnt = [_bits(_wmask(info, topo, plane, (p - (sl * NC + k)) % n, sl * NC + k)) for sl in range(SLOTS)]
     sent = [0]
@@ -173,6 +192,7 @@ def _compute_core(g, c, T, topo, info):
         first = big if sl == SLOTS - 1 else 0
         units += [(sl, first), (sl, 1 - first)]
 
+    _ident_block(g, c, T, topo, k, R, sent)
     g.wait_ge(S.xo, xcnt[0])
     _send(g, topo, peer, T.xm[:, :wid[0]], T.xo[:, :wid[0]], S.xm, S.snt, ym, sent)
     for sl in range(SLOTS):
@@ -188,42 +208,40 @@ def _compute_core(g, c, T, topo, info):
         g.wait_ge(sem, 1)
         dst = mateR if q else R
         i = 2 * k + q
-        _send(g, topo, dst, T["part%d" % i][:, :wid[q]], YB[q][:, :wid[q]], S["pa%d" % i], S.snt, ym, sent)
+        _send(g, topo, dst, T["part%d" % i][:, :wid[q]], YB[q][:, :wid[q]], S["pa%d" % i], S.snt,
+              _pmask(topo, info, c, q), sent)
     g.wait_ge(S.snt, sent[0])
 
-    def z(u):
+    def zb(u):
+        w = wid[units[u][1]]
+        if u < NU - 2:
+            return T["zz%d" % u][:, 0:w], T["zz%d" % u][:, TK:TK + w]
+        return T["za%d" % u][:, :w], T["zb%d" % u][:, :w]
+
+    for u in range(NU):
         sl, q = units[u]
-        w, b = wid[q], u % 2
+        w = wid[q]
         g.tensor.wait_ge(xsem[q], xcnt[q])
         g.tensor.wait_ge(S["ws%d" % sl], wcnt[sl])
-        if u >= 2:
-            g.tensor.wait_ge(S.hs, u - 1)
         W = T["wl%d" % sl]
-        g.tensor.matmul(T["z1%d" % b][:, :w], W[:, 0:D], X[q][:, :w], True, True).then_inc(S.z1s, 1)
-        g.tensor.matmul(T["z3%d" % b][:, :w], W[:, D:2 * D], X[q][:, :w], True, True).then_inc(S.z3s, 1)
-
-    def y(u):
+        g.tensor.matmul(zb(u)[0], W[:, 0:D], X[q][:, :w], True, True).then_inc(S.z1s, 1)
+        g.tensor.matmul(zb(u)[1], W[:, D:2 * D], X[q][:, :w], True, True).then_inc(S.z3s, 1)
+    for u in range(NU):
         sl, q = units[u]
         w = wid[q]
         g.tensor.wait_ge(S.hs, u + 1)
         g.tensor.matmul(YP[q][:, :w], T["wl%d" % sl][:, 2 * D:3 * D], T["h%d" % u][:, :w],
                         sl == 0, sl == SLOTS - 1).then_inc(S.ys, 1)
 
-    for sl in range(SLOTS):
-        z(2 * sl)
-        z(2 * sl + 1)
-        y(2 * sl)
-        y(2 * sl + 1)
-
     for u in range(NU):
-        sl, q = units[u]
-        w, b = wid[q], u % 2
+        w = wid[units[u][1]]
         g.scalar.wait_ge(S.z1s, u + 1)
-        g.scalar.activation(T["s%d" % u][:, :w], T["z1%d" % b][:, :w], ActivationFunctionType.Silu).then_inc(S.ss, 1)
+        if u < NU - 2:
+            g.scalar.wait_ge(S.z3s, u + 1)
+        g.scalar.activation(T["s%d" % u][:, :w], zb(u)[0], ActivationFunctionType.Silu).then_inc(S.ss, 1)
         g.vector.wait_ge(S.ss, u + 1)
         g.vector.wait_ge(S.z3s, u + 1)
-        g.vector.tensor_tensor(T["h%d" % u][:, :w], T["s%d" % u][:, :w], T["z3%d" % b][:, :w],
-                               AluOpType.mult).then_inc(S.hs, 1)
+        g.vector.tensor_tensor(T["h%d" % u][:, :w], T["s%d" % u][:, :w], zb(u)[1], AluOpType.mult).then_inc(S.hs, 1)
     g.scalar.wait_ge(S.ys, NU - 1)
     g.scalar.activation(YB[big][:, :wid[big]], YP[big][:, :wid[big]], ActivationFunctionType.Copy).then_inc(S.yca, 1)
     g.vector.wait_ge(S.ys, NU)

from concourse.bass import DstId, RemoteDMATransfer
from concourse.mybir import AluOpType, ActivationFunctionType
import comms_topo

CORES = [32, 40, 48, 56, 64, 72, 80, 88, 96, 104, 112, 120]
D = 128
TK = 256
NC = 3
IB = D // (NC + 1)
FWD = {4: 0, 5: 1}
NSET = 1 + sum(1 for c in CORES[1:] if comms_topo.same_plane(comms_topo.chip(CORES[0]), comms_topo.chip(c)))
SLOTS = NSET // NC
NU = 2 * SLOTS

SCRATCH = {
    "x0": ("sbuf", [D, TK], "bfloat16"),
    "wown": ("sbuf", [D, 3 * D], "bfloat16"),
    "ident": ("sbuf", [D, D], "bfloat16"),
    "yout": ("sbuf", [D, TK], "bfloat16"),
    "ones": ("sbuf", [D, IB], "bfloat16"),
    "idb": ("sbuf", [D, IB], "bfloat16"),
    "yp0": ("psum", [D, 512], "float32"),
    "xo": ("sbuf", [D, TK], "bfloat16"),
    "xm": ("sbuf", [D, TK], "bfloat16"),
    "yb0": ("sbuf", [D, TK], "bfloat16"),
    "yb1": ("sbuf", [D, TK], "bfloat16"),
    "yp1": ("psum", [D, 512], "float32"),
}
for _i in range(2 * NC):
    SCRATCH["part%d" % _i] = ("sbuf", [D, TK], "bfloat16")
for _i in range(SLOTS):
    SCRATCH["wl%d" % _i] = ("sbuf", [D, 3 * D], "bfloat16")
for _i in range(NU):
    if _i < NU - 2:
        SCRATCH["zz%d" % _i] = ("psum", [D, 512], "float32")
    else:
        SCRATCH["za%d" % _i] = ("psum", [D, 512], "float32")
        SCRATCH["zb%d" % _i] = ("psum", [D, 512], "float32")
    SCRATCH["s%d" % _i] = ("sbuf", [D, TK], "float32")
    SCRATCH["h%d" % _i] = ("sbuf", [D, TK], "bfloat16")

SEMAPHORES = (["lx", "lw", "idm", "ids", "idr", "snt", "acc", "cp", "st", "xo", "xm",
               "z1s", "z3s", "ss", "hs", "ys", "yca", "ycb"]
              + ["pa%d" % i for i in range(2 * NC)] + ["ws%d" % i for i in range(SLOTS)])


def _bits(m):
    return bin(m).count("1")


def _plan(T, topo):
    cores = list(T.cores)
    info = {}
    for r, R in enumerate(cores):
        ch = topo.chip(R)
        mate = [q for q in cores if topo.mates(ch, topo.chip(q))][0]
        plane = [q for q in cores if q == R or topo.same_plane(ch, topo.chip(q))]
        own = [c for c in range(topo.CHIPS * topo.CORES_PER_CHIP)
               if topo.chip(c) == ch and c != R and topo.may_write(c, mate)]
        own.sort(key=lambda c: (topo.die(c) == topo.die(R), c))
        info[R] = {"rank": r, "mate": mate, "plane": plane, "comp": own[:NC]}
    return info


def _where(info, plane, j, s):
    q = plane[(j + s) % len(plane)]
    return info[q]["comp"][s % NC], s // NC


def _wmask(info, topo, plane, j, s):
    dst = _where(info, plane, j, s)[0]
    if s == 0:
        return topo.mask(plane[j], dst) & ~topo.mask(plane[j], info[plane[j]]["mate"])
    src = _where(info, plane, j, FWD[s])[0] if s in FWD else plane[j]
    return topo.mask(src, dst)


def _send(g, topo, dst, out_ap, in_ap, rsem, lsem, mask, sent):
    rid, pid, _ = topo.addr(dst)
    g.remote_dma(out_ap=out_ap, in_ap=in_ap, remote_sem=rsem, local_sem=lsem, pid=pid, routing_id=rid,
                 dma_engine_mask=mask)
    sent[0] += _bits(mask)


def _ident_block(g, me, T, topo, b, dst, sent):
    S = T.sem
    g.vector.memset(T.ones[:, :], 1.0).then_inc(S.idm, 1)
    g.wait_ge(S.idm, 1)
    g.affine_select(T.idb[:, :], T.ones[:, :], [[-1, IB]], AluOpType.is_equal, 0.0, -b * IB, 1).then_inc(S.ids, 1)
    g.wait_ge(S.ids, 1)
    _send(g, topo, dst, T.ident[:, b * IB:(b + 1) * IB], T.idb[:, :], S.idr, S.snt, topo.mask(me, dst), sent)


def _rank_core(g, R, T, topo, info):
    S = T.sem
    me = info[R]
    wid = T.tables["WID"][me["rank"]]
    comp, plane = me["comp"], me["plane"]
    n, p = len(plane), plane.index(R)
    sent = [0]

    g.sync.dma_start(T.x0[:, :wid], T.x[:, :wid]).then_inc(S.lx, 16)
    g.scalar.dma_start(T.wown[:, 0:D], T.w1[:, :]).then_inc(S.lw, 16)
    g.sync.dma_start(T.wown[:, D:2 * D], T.w3[:, :]).then_inc(S.lw, 16)
    g.scalar.dma_start(T.wown[:, 2 * D:3 * D], T.w2[:, :]).then_inc(S.lw, 16)

    _ident_block(g, R, T, topo, NC, plane[(p + 1) % n], sent)

    xmask = topo.mask(R, comp[0])
    g.wait_ge(S.lx, 16)
    ids = []
    for c in comp:
        rid, pid, _ = topo.addr(c)
        ids.append(DstId(rid=rid, pnc=pid))
    g.remote_dma_fused([RemoteDMATransfer(dst_ids=ids, dma_engine_mask=xmask, remote_sem=S.xo,
                                          srcs=[T.x0[:, :wid]], dsts=[T.xo[:, :wid]] * len(comp))],
                       local_sem=S.snt)
    sent[0] += _bits(xmask)

    g.wait_ge(S.lw, 48)
    direct = [s for s in range(1, n) if s not in FWD]
    trs = []
    for s in (0, direct[0]):
        c, sl = _where(info, plane, p, s)
        rid, pid, _ = topo.addr(c)
        m = _wmask(info, topo, plane, p, s)
        trs.append(RemoteDMATransfer(dst_ids=[DstId(rid=rid, pnc=pid)], dma_engine_mask=m,
                                     remote_sem=S["ws%d" % sl], srcs=[T.wown[:, :]], dsts=[T["wl%d" % sl][:, :]]))
        sent[0] += _bits(m)
    g.remote_dma_fused(trs, local_sem=S.snt)
    for s in direct[1:]:
        c, sl = _where(info, plane, p, s)
        _send(g, topo, c, T["wl%d" % sl][:, :], T.wown[:, :], S["ws%d" % sl], S.snt,
              _wmask(info, topo, plane, p, s), sent)

    def _pcnt(i):
        src = info[me["mate"]]["comp"][i // 2] if i % 2 else comp[i // 2]
        return _bits(_pmask(topo, info, src, i % 2))

    order = [2 * k for k in range(NC)] + [2 * k + 1 for k in range(NC)]
    g.tensor.wait_ge(S.idr, sum(_bits(topo.mask(c, R)) for c in comp + [plane[(p - 1) % n]]))
    for n_, i in enumerate(order[:-1]):
        g.tensor.wait_ge(S["pa%d" % i], _pcnt(i))
        mm = g.tensor.matmul(T.yp0[:, :wid], T.ident[:, :], T["part%d" % i][:, :wid], n_ == 0, n_ == len(order) - 2)
    mm.then_inc(S.acc, 1)
    last = order[-1]
    g.vector.wait_ge(S["pa%d" % last], _pcnt(last))
    g.vector.wait_ge(S.acc, 1)
    g.vector.tensor_tensor(T.yout[:, :wid], T.yp0[:, :wid], T["part%d" % last][:, :wid], AluOpType.add).then_inc(S.cp, 1)
    g.sync.wait_ge(S.cp, 1)
    g.sync.dma_start(T.y[:, :wid], T.yout[:, :wid]).then_inc(S.st, 16)
    g.sync.wait_ge(S.st, 16)
    g.wait_ge(S.snt, sent[0])


def _home(topo, info, c):
    return [R for R in info if topo.chip(R) == topo.chip(c)][0]


def _ymask(topo, info, c):
    R = _home(topo, info, c)
    return topo.mask(c, R) & topo.mask(c, info[R]["mate"])


def _pmask(topo, info, c, far):
    R = _home(topo, info, c)
    return _ymask(topo, info, c) if far else topo.mask(c, R) & ~topo.mask(c, info[R]["mate"])


def _compute_core(g, c, T, topo, info):
    S = T.sem
    R = _home(topo, info, c)
    me = info[R]
    k = me["comp"].index(c)
    plane = me["plane"]
    n, p = len(plane), plane.index(R)
    mateR = me["mate"]
    peer = info[mateR]["comp"][k]
    wid = (T.tables["WID"][me["rank"]], T.tables["WID"][info[mateR]["rank"]])
    X = (T.xo, T.xm)
    YP = (T.yp0, T.yp1)
    YB = (T.yb0, T.yb1)
    ym = _ymask(topo, info, c)
    xcnt = (_bits(topo.mask(R, c)), _bits(_ymask(topo, info, peer)))
    xsem = (S.xo, S.xm)
    wcnt = [_bits(_wmask(info, topo, plane, (p - (sl * NC + k)) % n, sl * NC + k)) for sl in range(SLOTS)]
    sent = [0]

    big = 0 if wid[0] >= wid[1] else 1
    units = []
    for sl in range(SLOTS):
        first = big if sl == SLOTS - 1 else 0
        units += [(sl, first), (sl, 1 - first)]

    _ident_block(g, c, T, topo, k, R, sent)
    g.wait_ge(S.xo, xcnt[0])
    _send(g, topo, peer, T.xm[:, :wid[0]], T.xo[:, :wid[0]], S.xm, S.snt, ym, sent)
    for sl in range(SLOTS):
        held = sl * NC + k
        j = (p - held) % n
        for s in sorted(FWD):
            if FWD[s] == held:
                dst, dsl = _where(info, plane, j, s)
                g.wait_ge(S["ws%d" % sl], wcnt[sl])
                _send(g, topo, dst, T["wl%d" % dsl][:, :], T["wl%d" % sl][:, :], S["ws%d" % dsl], S.snt,
                      _wmask(info, topo, plane, j, s), sent)
    for q, sem in ((big, S.yca), (1 - big, S.ycb)):
        g.wait_ge(sem, 1)
        dst = mateR if q else R
        i = 2 * k + q
        _send(g, topo, dst, T["part%d" % i][:, :wid[q]], YB[q][:, :wid[q]], S["pa%d" % i], S.snt,
              _pmask(topo, info, c, q), sent)
    g.wait_ge(S.snt, sent[0])

    def zb(u):
        w = wid[units[u][1]]
        if u < NU - 2:
            return T["zz%d" % u][:, 0:w], T["zz%d" % u][:, TK:TK + w]
        return T["za%d" % u][:, :w], T["zb%d" % u][:, :w]

    for u in range(NU):
        sl, q = units[u]
        w = wid[q]
        g.tensor.wait_ge(xsem[q], xcnt[q])
        g.tensor.wait_ge(S["ws%d" % sl], wcnt[sl])
        W = T["wl%d" % sl]
        g.tensor.matmul(zb(u)[0], W[:, 0:D], X[q][:, :w], True, True).then_inc(S.z1s, 1)
        g.tensor.matmul(zb(u)[1], W[:, D:2 * D], X[q][:, :w], True, True).then_inc(S.z3s, 1)
    for u in range(NU):
        sl, q = units[u]
        w = wid[q]
        g.tensor.wait_ge(S.hs, u + 1)
        g.tensor.matmul(YP[q][:, :w], T["wl%d" % sl][:, 2 * D:3 * D], T["h%d" % u][:, :w],
                        sl == 0, sl == SLOTS - 1).then_inc(S.ys, 1)

    for u in range(NU):
        w = wid[units[u][1]]
        g.scalar.wait_ge(S.z1s, u + 1)
        if u < NU - 2:
            g.scalar.wait_ge(S.z3s, u + 1)
        g.scalar.activation(T["s%d" % u][:, :w], zb(u)[0], ActivationFunctionType.Silu).then_inc(S.ss, 1)
        g.vector.wait_ge(S.ss, u + 1)
        g.vector.wait_ge(S.z3s, u + 1)
        g.vector.tensor_tensor(T["h%d" % u][:, :w], T["s%d" % u][:, :w], zb(u)[1], AluOpType.mult).then_inc(S.hs, 1)
    g.scalar.wait_ge(S.ys, NU - 1)
    g.scalar.activation(YB[big][:, :wid[big]], YP[big][:, :wid[big]], ActivationFunctionType.Copy).then_inc(S.yca, 1)
    g.vector.wait_ge(S.ys, NU)
    g.vector.tensor_copy(YB[1 - big][:, :wid[1 - big]], YP[1 - big][:, :wid[1 - big]]).then_inc(S.ycb, 1)


def rank_program(g, core, T, topo):
    info = _plan(T, topo)
    if core in info:
        _rank_core(g, core, T, topo, info)
        return
    for R in info:
        if core in info[R]["comp"]:
            _compute_core(g, core, T, topo, info)
            return
